import numpy as np
import ml_dtypes


def mxq(x, axis, fmt="e4m3"):
    dtype, down = {"e4m3": (ml_dtypes.float8_e4m3fn, 7), "e5m2": (ml_dtypes.float8_e5m2, 14)}[fmt]
    v = np.moveaxis(np.asarray(x, np.float32).astype(ml_dtypes.bfloat16).astype(np.float64), axis, -1)
    blocks = v.reshape(v.shape[:-1] + (-1, 32))
    amax = np.abs(blocks).max(-1, keepdims=True)
    byte = np.maximum(np.where(amax > 0, np.frexp(amax)[1] - 1 + 127, 0) - down, 1)
    scale = np.exp2(byte - 127.0)
    codes = (blocks / scale).astype(np.float32).astype(dtype).astype(np.float64)
    return np.moveaxis((codes * scale).reshape(v.shape), -1, axis)


WIDE = False


def mx_kscale(k):
    if not WIDE:
        return np.ones(k)
    levels = np.array([10, -10, 5, -5, 0])
    if k % 512:
        return np.exp2(np.random.permutation(np.resize(levels, k // 32))).repeat(32)
    a = np.empty((k // 512, 16))
    for p in range(k // 512):
        a[p, :8] = np.random.permutation(np.resize(levels, 8))
        for g in range(8):
            far = levels[np.abs(levels - a[p, g]) >= 10]
            a[p, g + 8] = far[np.random.randint(len(far))]
    return np.exp2(a.ravel()).repeat(32)


def f64(x):
    return np.asarray(x).astype(np.float64)


def striped(idx):
    return np.tile(idx.reshape(-1, 16).T, (8, 1)).astype(np.uint16)


def unstriped(offs):
    return offs[:16].T.reshape(-1).astype(np.int64)


def striped8(idx):
    return np.concatenate([x.reshape(-1, 16).T for x in idx]).astype(np.uint16)


def runs(offs, k):
    lists = np.stack([offs[16 * r : 16 * r + 16].T.reshape(-1) for r in range(8)]).astype(np.int64)
    return lists[np.arange(k) % 512 // 64]


def pack_weight(w):
    k, n = w.shape
    w = f64(np.asarray(w, np.float32).astype(ml_dtypes.bfloat16)).reshape(k // 32, 32, n)
    amax = np.abs(w).max(1)
    byte = np.clip(np.where(amax > 0, np.frexp(amax)[1] - 1 + 127 - 7, 1), 1, 254)
    scaled = (w * np.exp2(127.0 - byte)[:, None, :]).reshape(k, n).astype(np.float32)
    words = np.ascontiguousarray(scaled.reshape(k // 512, 128, 4, n).transpose(0, 1, 3, 2)).astype(ml_dtypes.float8_e4m3fn).view(np.uint8)
    return words, np.ascontiguousarray(byte.astype(np.uint8).reshape(k // 512, 16, n))


def unpack_weight(words, scales):
    g, p, n, _ = words.shape
    vals = np.ascontiguousarray(words).view(ml_dtypes.float8_e4m3fn).astype(np.float64) * np.repeat(np.exp2(scales.astype(np.float64) - 127.0), 8, axis=1)[..., None]
    return vals.transpose(0, 1, 3, 2).reshape(g * 512, n)


def sigmoid(v):
    return 1.0 / (1.0 + np.exp(-np.maximum(v, -700.0)))


K, T, S, G, H, J = 512, 2048, 512, 2048, 512, 512


def setup_inputs():
    n = np.random.standard_normal
    s = mx_kscale(K)[:, None]
    packed_xT = pack_weight(n((K, T)) * s)
    packed_dT = pack_weight(n((K, G)) / s)
    return {
        "x_words": packed_xT[0],
        "x_scales": packed_xT[1],
        "d_words": packed_dT[0],
        "d_scales": packed_dT[1],
        "tab": n((H, J)).astype(np.float32),
        "sl": np.random.uniform(1.0, 2.0, (H, 1)).astype(np.float32),
        "th": (0.5 * n((H, 1))).astype(np.float32),
        "gs": (np.random.uniform(0.5, 1.5, (K, 1)) * s).astype(np.float32),
        "tau": np.random.uniform(0.3, 0.9, (H, 1)).astype(np.float32),
        "offs": striped(np.random.permutation(T)[:S]),
        "k1": striped8(np.random.randint(0, G, (8, H))),
        "n1": striped(np.random.randint(0, J, S)),
        "n2": striped(np.random.permutation(S)),
        "n3": striped8(np.stack([np.random.permutation(S) for _ in range(8)])),
    }


def reference(x_words, x_scales, d_words, d_scales, tab, sl, th, gs, tau, offs, k1, n1, n2, n3):
    d_k1 = unpack_weight(d_words, d_scales)[np.arange(K)[:, None], runs(k1, K)]
    xq = unpack_weight(x_words, x_scales)[:, unstriped(offs)]
    h = 0.0625 * (d_k1.T @ xq)
    sg = sigmoid(f64(sl) * (f64(tab)[:, unstriped(n1)] - f64(th)))
    z = f64(gs) * (h * sg - (0.5 * h[:, unstriped(n2)]))
    h2 = 0.0625 * ((d_k1.T @ mxq(z, 0, "e4m3")))
    top = h2.max(axis=1, keepdims=True)
    ea = np.exp(f64(tau) * (h2[np.arange(H)[:, None], runs(n3, H)] - top))
    return 2.0 * (h2 * ea)

from contextlib import ExitStack

import concourse.mybir as mybir

K, T, S, G, H, J = 512, 2048, 512, 2048, 512, 512
FLOPS = 2 * (2 * K * H * S)

F32 = mybir.dt.float32
BF16 = mybir.dt.bfloat16
I32 = mybir.dt.int32
U32 = mybir.dt.uint32
U16 = mybir.dt.uint16
U8 = mybir.dt.uint8
FP8X4 = mybir.dt.float8_e4m3fn_x4
ALU = mybir.AluOpType
ACT = mybir.ActivationFunctionType

P = 128
PACK = 4
HALF = 256
Z_CHUNKS = ((0, 256), (256, 384), (384, 512))


def entries(offsets, j0, j1):
    return offsets[:, j0 // 16 : j1 // 16]


def tile_picked_ringekdepk_none_p_kernel(
    tc, x_words, x_scales, d_words, d_scales, tab, sl, th, gs, tau, offs, k1, n1, n2, n3, out
):
    nc = tc.nc
    with ExitStack() as ctx:
        lists = ctx.enter_context(tc.tile_pool(name="lists", bufs=1))
        sb = ctx.enter_context(tc.tile_pool(name="sb", bufs=1))
        psum = ctx.enter_context(tc.psum_pool(name="psum", bufs=1))

        def list_tile(name):
            return lists.tile([P, S // 16], U16, name=name)

        k1_sb, offs_sb, n1_sb, n2_sb, n3_sb = (list_tile(n) for n in ("k1_sb", "offs_sb", "n1_sb", "n2_sb", "n3_sb"))

        def row_tile(name):
            return sb.tile([P, PACK], F32, name=name)

        sl_sb, th_sb, gs_sb, tau_sb = (row_tile(n) for n in ("sl_sb", "th_sb", "gs_sb", "tau_sb"))

        d_scale_win = sb.tile([P, G], U8, name="d_scale_win", align_bytes=64)
        x_scale_win = sb.tile([P, T], U8, name="x_scale_win", align_bytes=64)
        d_word_win = sb.tile([P, G], U32, name="d_word_win", align_bytes=64)
        x_word_win = sb.tile([P, T], U32, name="x_word_win", align_bytes=64)
        tab_sb = [sb.tile([P, J], F32, name=f"tab{t}") for t in range(PACK)]
        tab_rows = tab.rearrange("(p t) j -> t p j", t=PACK)
        out_rows = out.rearrange("(p t) j -> t p j", t=PACK)

        def load_rows(queue, vec_sb, vec):
            queue.dma_start(vec_sb[:], vec.rearrange("(p t) o -> p (t o)", t=PACK))

        nc.gpsimd.memset(d_scale_win[:].bitcast(I32), 0)
        nc.vector.memset(x_scale_win[:].bitcast(I32), 0)
        nc.sync.dma_start(k1_sb[:], k1)
        nc.sync.dma_start(n1_sb[:], n1)
        nc.sync.dma_start(tab_sb[0][:], tab_rows[0])
        for e in range(2):
            nc.sync.dma_start(d_scale_win[e:P:16, :].bitcast(I32), d_scales[0, e:16:2, :].bitcast(I32))
        load_rows(nc.scalar, sl_sb, sl)
        load_rows(nc.scalar, th_sb, th)
        nc.sync.dma_start(d_word_win[:].bitcast(I32), d_words[0].rearrange("p n r -> p (n r)").bitcast(I32))
        nc.sync.dma_start(offs_sb[:], offs)
        nc.sync.dma_start(tab_sb[1][:], tab_rows[1])
        for q in range(4):
            nc.scalar.dma_start(
                x_scale_win[32 * q : 32 * q + 4, :].bitcast(I32), x_scales[0, 4 * q : 4 * q + 4, :].bitcast(I32)
            )
        nc.sync.dma_start(x_word_win[:].bitcast(I32), x_words[0].rearrange("p n r -> p (n r)").bitcast(I32))
        load_rows(nc.sync, gs_sb, gs)
        for t in range(2, PACK):
            nc.sync.dma_start(tab_sb[t][:], tab_rows[t])
        nc.sync.dma_start(n2_sb[:], n2)
        nc.sync.dma_start(n3_sb[:], n3)
        load_rows(nc.sync, tau_sb, tau)

        d_scale_got = sb.tile([P, H], U8, name="d_scale_got", align_bytes=64)
        d_scale_dealt = sb.tile([P, H], U8, name="d_scale_dealt", align_bytes=64)
        d_scale = sb.tile([P, H], U8, name="d_scale", align_bytes=64)
        nc.vector.tensor_copy(d_scale_got[:], d_scale_win[:].indirect(k1_sb[:]))
        for dealt in (d_scale_dealt, d_scale):
            nc.vector.tensor_copy(
                dealt[:].rearrange("p (t m) -> p t m", t=PACK), d_scale_got[:].rearrange("p (m t) -> p t m", t=PACK)
            )
        for e in range(2):
            nc.scalar.dma_start(d_scale[2 + e : P : 32, :].bitcast(I32), d_scale_dealt[16 + e : P : 32, :].bitcast(I32))

        sg_bias = row_tile("sg_bias")
        nc.vector.scalar_tensor_tensor(sg_bias[:], sl_sb[:], -1.0, th_sb[:], ALU.mult, ALU.mult)

        x_scale = sb.tile([P, S], U8, name="x_scale", align_bytes=64)
        nc.vector.tensor_copy(x_scale[:], x_scale_win[:].indirect(offs_sb[:]))

        d_word_got = sb.tile([P, H], U32, name="d_word_got", align_bytes=64)
        d_word = sb.tile([P, H], U32, name="d_word", align_bytes=64)
        nc.vector.tensor_copy(d_word_got[:], d_word_win[:].indirect(k1_sb[:]))
        nc.vector.tensor_copy(
            d_word[:].rearrange("p (t m) -> p t m", t=PACK), d_word_got[:].rearrange("p (m t) -> p t m", t=PACK)
        )
        x_word = [sb.tile([P, HALF], U32, name=f"x_word{c}", align_bytes=64) for c in range(2)]
        for c in range(2):
            nc.vector.tensor_copy(x_word[c][:], x_word_win[:].indirect(entries(offs_sb, c * HALF, (c + 1) * HALF)))

        def product(acc, t, words, scales):
            nc.tensor.matmul_mx(
                out=acc,
                lhsT=d_word[:, t * P : (t + 1) * P].bitcast(FP8X4),
                lhsT_scale=d_scale[:, t * P : (t + 1) * P],
                rhs=words.bitcast(FP8X4),
                rhs_scale=scales,
                start=True,
                stop=True,
            )

        sg = [sb.tile([P, S], F32, name=f"sg{t}") for t in range(PACK)]
        for t in range(PACK):
            for c in range(2):
                nc.scalar.activation(
                    sg[t][:, c * HALF : (c + 1) * HALF],
                    tab_sb[t][:].indirect(entries(n1_sb, c * HALF, (c + 1) * HALF)),
                    ACT.Sigmoid,
                    bias=sg_bias[:, t : t + 1],
                    scale=sl_sb[:, t : t + 1],
                )

        h_acc = [psum.tile([P, S], F32, name=f"h_acc{t}", tag=f"first{t}") for t in range(PACK)]
        for t, c in ((0, 0), (1, 0), (0, 1), (1, 1), (2, 0), (2, 1), (3, 0), (3, 1)):
            cols = slice(c * HALF, (c + 1) * HALF)
            product(h_acc[t][:, cols], t, x_word[c][:], x_scale[:, cols])

        u = [sb.tile([P, S], F32, name=f"u{t}") for t in range(PACK)]
        for t in range(PACK):
            nc.vector.tensor_scalar(u[t][:], h_acc[t][:], gs_sb[:, t : t + 1], 0.03125, ALU.mult, ALU.mult)
        gated = sb.tile([P, PACK, S], F32, name="gated")
        for t in range(PACK):
            nc.vector.scalar_tensor_tensor(gated[:, t, :], u[t][:], 2.0, sg[t][:], ALU.mult, ALU.mult)

        fetched = [sb.tile([P, PACK, j1 - j0], F32, name=f"fetched{j0}") for j0, j1 in Z_CHUNKS]
        for (j0, j1), f in zip(Z_CHUNKS, fetched):
            for t in range(PACK):
                nc.scalar.activation(f[:, t, :], u[t][:].indirect(entries(n2_sb, j0, j1)), ACT.Copy)

        z = [sb.tile([P, j1 - j0, PACK], BF16, name=f"z{j0}", align_bytes=64) for j0, j1 in Z_CHUNKS]
        z_word = [sb.tile([P, j1 - j0], U32, name=f"z_word{j0}", align_bytes=64) for j0, j1 in Z_CHUNKS]
        z_scale = [sb.tile([P, j1 - j0], U8, name=f"z_scale{j0}", align_bytes=64) for j0, j1 in Z_CHUNKS]
        h2_acc = [psum.tile([P, S], F32, name=f"h2_acc{t}", tag=f"second{t}") for t in range(PACK)]
        h2_last = psum.tile([P, P], F32, name="h2_last", tag="first0")

        def make_z(c):
            j0, j1 = Z_CHUNKS[c]
            nc.vector.tensor_tensor(
                z[c][:].rearrange("p (c i) t -> p c t i", i=4),
                gated[:, :, j0:j1].rearrange("p t (c i) -> p c t i", i=4),
                fetched[c][:].rearrange("p t (c i) -> p c t i", i=4),
                ALU.subtract,
            )

        def quantise_and_multiply(c):
            j0, j1 = Z_CHUNKS[c]
            nc.vector.quantize_mx(
                out=z_word[c][:].bitcast(FP8X4), scales=z_scale[c][:], in_=z[c][:].rearrange("p w t -> p (w t)")
            )
            for t in range(PACK):
                acc = h2_last[:] if (t == 0 and j1 == S) else h2_acc[t][:, j0:j1]
                product(acc, t, z_word[c][:], z_scale[c][:])

        make_z(0)
        make_z(1)
        quantise_and_multiply(0)
        make_z(2)
        quantise_and_multiply(1)
        quantise_and_multiply(2)

        h2 = [sb.tile([P, S], F32, name=f"h2_{t}") for t in range(PACK)]
        ea = [sb.tile([P, S], F32, name=f"ea{t}") for t in range(PACK)]
        res = [sb.tile([P, S], F32, name=f"res{t}") for t in range(PACK)]
        top_part = sb.tile([P, 1], F32, name="top_part")
        top = row_tile("top")
        ea_bias = row_tile("ea_bias")
        split = Z_CHUNKS[-1][0]

        def leave_psum(t):
            col = slice(t, t + 1)
            if t == 0:
                nc.vector.tensor_scalar(
                    h2[0][:, :split], h2_acc[0][:, :split], 0.0625, None, ALU.mult, ALU.max, accum_out=top_part[:]
                )
                nc.vector.tensor_scalar(
                    h2[0][:, split:], h2_last[:], 0.0625, top_part[:], ALU.mult, ALU.max, accum_out=top[:, col]
                )
            else:
                nc.vector.tensor_scalar(h2[t][:], h2_acc[t][:], 0.0625, None, ALU.mult, ALU.max, accum_out=top[:, col])
            nc.vector.tensor_scalar(ea_bias[:, col], top[:, col], tau_sb[:, col], -1.0, ALU.mult, ALU.mult)

        def finish(t):
            col = slice(t, t + 1)
            for c in range(2):
                cols = slice(c * HALF, (c + 1) * HALF)
                nc.scalar.activation(
                    ea[t][:, cols],
                    h2[t][:].indirect(entries(n3_sb, c * HALF, (c + 1) * HALF)),
                    ACT.Exp,
                    bias=ea_bias[:, col],
                    scale=tau_sb[:, col],
                )
            pieces = (slice(0, S),) if t < PACK - 1 else (slice(0, HALF), slice(HALF, S))
            for cols in pieces:
                nc.vector.scalar_tensor_tensor(res[t][:, cols], h2[t][:, cols], 2.0, ea[t][:, cols], ALU.mult, ALU.mult)
                nc.sync.dma_start(out_rows[t][:, cols], res[t][:, cols])

        leave_psum(0)
        leave_psum(1)
        finish(0)
        leave_psum(2)
        finish(1)
        leave_psum(3)
        finish(2)
        finish(3)
